import numpy as np
import ml_dtypes


def mxq(x, axis, fmt="e4m3"):
    dtype, down = {"e4m3": (ml_dtypes.float8_e4m3fn, 7), "e5m2": (ml_dtypes.float8_e5m2, 14)}[fmt]
    v = np.moveaxis(np.asarray(x, np.float32).astype(ml_dtypes.bfloat16).astype(np.float64), axis, -1)
    blocks = v.reshape(v.shape[:-1] + (-1, 32))
    amax = np.abs(blocks).max(-1, keepdims=True)
    byte = np.maximum(np.where(amax > 0, np.frexp(amax)[1] - 1 + 127, 0) - down, 1)
    scale = np.exp2(byte - 127.0)
    codes = (blocks / scale).astype(np.float32).astype(dtype).astype(np.float64)
    return np.moveaxis((codes * scale).reshape(v.shape), -1, axis)


WIDE = False


def mx_kscale(k):
    if not WIDE:
        return np.ones(k)
    levels = np.array([10, -10, 5, -5, 0])
    if k % 512:
        return np.exp2(np.random.permutation(np.resize(levels, k // 32))).repeat(32)
    a = np.empty((k // 512, 16))
    for p in range(k // 512):
        a[p, :8] = np.random.permutation(np.resize(levels, 8))
        for g in range(8):
            far = levels[np.abs(levels - a[p, g]) >= 10]
            a[p, g + 8] = far[np.random.randint(len(far))]
    return np.exp2(a.ravel()).repeat(32)


def f64(x):
    return np.asarray(x).astype(np.float64)


def striped(idx):
    return np.tile(np.asarray(idx).reshape(-1, 16).T, (8, 1)).astype(np.uint16)


def unstriped(offs):
    return offs[:16].T.reshape(-1).astype(np.int64)


E2M1 = np.array([0.0, 0.5, 1.0, 1.5, 2.0, 3.0, 4.0, 6.0, -0.0, -0.5, -1.0, -1.5, -2.0, -3.0, -4.0, -6.0])


def pack_weight(w, fmt):
    k, n = w.shape
    w = f64(np.asarray(w, np.float32).astype(ml_dtypes.bfloat16)).reshape(k // 32, 32, n)
    amax = np.abs(w).max(1)
    if fmt == "e4m3":
        byte = np.frexp(amax)[1] - 1 + 127 - 7
    else:
        mant, ex = np.frexp(amax / 6.0)
        byte = np.where(mant > 0.5, ex, ex - 1) + 127
    byte = np.clip(np.where(amax > 0, byte, 1), 1, 254)
    scaled = (w * np.exp2(127.0 - byte)[:, None, :]).reshape(k, n).astype(np.float32)
    by_word = np.ascontiguousarray(scaled.reshape(k // 512, 128, 4, n).transpose(0, 1, 3, 2))
    if fmt == "e4m3":
        words = by_word.astype(ml_dtypes.float8_e4m3fn).view(np.uint8)
    else:
        c = by_word.astype(ml_dtypes.float4_e2m1fn).view(np.uint8) & 0xF
        words = (c[..., 0::2] | (c[..., 1::2] << 4)).reshape(k // 512, 128, 2 * n)
    return np.ascontiguousarray(words), np.ascontiguousarray(byte.astype(np.uint8).reshape(k // 512, 16, n))


def unpack_weight(words, scales, fmt):
    g, _, n = scales.shape
    words = np.ascontiguousarray(words).reshape(g, 128, n, -1)
    if fmt == "e4m3":
        vals = words.view(ml_dtypes.float8_e4m3fn).astype(np.float64)
    else:
        nib = np.empty((g, 128, n, 4), np.uint8)
        nib[..., 0::2] = words & 0xF
        nib[..., 1::2] = words >> 4
        vals = E2M1[nib]
    vals = vals * np.repeat(np.exp2(scales.astype(np.float64) - 127.0), 8, axis=1)[..., None]
    return vals.transpose(0, 1, 3, 2).reshape(g * 512, n)


D, K, U, I, E = 512, 512, 1024, 512, 256


def setup_inputs():
    n = np.random.standard_normal
    idx = np.random.permutation(U)[:I]
    idx2 = np.random.permutation(U)[:I]
    idx3 = np.random.permutation(U)[:I]
    fd = mx_kscale(D)
    fk = mx_kscale(K)
    notesp = pack_weight(n((D, U)) / fd[:, None], "e2m1")
    wbp = pack_weight(n((D, K)) * 1.0 / np.sqrt(D) * fd[:, None], "e4m3")
    wop = pack_weight(n((K, E)) * 1.0 / np.sqrt(K) / fk[:, None], "e2m1")
    return {
        "notes_words": notesp[0],
        "notes_scales": notesp[1],
        "wb_words": wbp[0],
        "wb_scales": wbp[1],
        "lam": (np.random.uniform(0.5, 1.5, (K, 1))).astype(np.float32),
        "kf": (np.random.uniform(0.5, 2.0, (K, 1)) * fk[:, None]).astype(np.float32),
        "wo_words": wop[0],
        "wo_scales": wop[1],
        "offs": striped(idx),
        "offs2": striped(idx2),
        "offs3": striped(idx3),
    }


def reference(notes_words, notes_scales, wb_words, wb_scales, lam, kf, wo_words, wo_scales, offs, offs2, offs3):
    idx = unstriped(offs)
    idx2 = unstriped(offs2)
    idx3 = unstriped(offs3)
    notesu = unpack_weight(notes_words, notes_scales, "e2m1")
    wbu = unpack_weight(wb_words, wb_scales, "e4m3")
    wou = unpack_weight(wo_words, wo_scales, "e2m1")
    h1 = wbu.T @ notesu
    f1 = np.zeros((K, U))
    f1[:, idx2] = h1[:, idx]
    c1 = h1 + f1 * f64(lam)
    v = c1[:, idx3] - h1[:, idx]
    w = v * f64(kf)
    wq = mxq(w, 0, "e4m3")
    y = wou.T @ wq
    return y

@@ -1,0 +1,208 @@
+from contextlib import ExitStack
+
+import concourse.mybir as mybir
+
+D, K, U, I, E = 512, 512, 1024, 512, 256
+P = 128
+PACK = 4
+BANK = 512
+HALF = I // 2
+FLOPS = 2 * D * K * U + 2 * K * E * I
+
+F32 = mybir.dt.float32
+BF16 = mybir.dt.bfloat16
+I32 = mybir.dt.int32
+U32 = mybir.dt.uint32
+U16 = mybir.dt.uint16
+U8 = mybir.dt.uint8
+FP8X4 = mybir.dt.float8_e4m3fn_x4
+FP4X4 = mybir.dt.float4_e2m1fn_x4
+MULT = mybir.AluOpType.mult
+ADD = mybir.AluOpType.add
+SUB = mybir.AluOpType.subtract
+COPY = mybir.ActivationFunctionType.Copy
+
+
+def tile_attend_hiddenhop_kernel(tc, notes_words, notes_scales, wb_words, wb_scales, lam, kf,
+                                  wo_words, wo_scales, offs, offs2, offs3, out):
+    nc = tc.nc
+    with ExitStack() as ctx:
+        keep = ctx.enter_context(tc.tile_pool(name="keep", bufs=1))
+        psum = ctx.enter_context(tc.psum_pool(name="psum", bufs=1))
+
+        def load_scale_rows(queue, plane, scales, quadrant):
+            queue.dma_start(out=plane[32 * quadrant : 32 * quadrant + 4, :].bitcast(I32),
+                            in_=scales[0, 4 * quadrant : 4 * quadrant + 4, :].bitcast(I32))
+
+        notes_codes = keep.tile([P, 2 * U], U8, align_bytes=64)
+        notes_plane = keep.tile([P, U], U8, align_bytes=64)
+        wb_raw_codes = keep.tile([P, K], U32, align_bytes=64)
+        wb_raw_plane = keep.tile([P, K], U8, align_bytes=64)
+        wo_codes = keep.tile([P, 2 * E], U8, align_bytes=64)
+        wo_plane = keep.tile([P, E], U8, align_bytes=64)
+        list1 = keep.tile([P, I // 16], U16)
+        list2 = keep.tile([P, I // 16], U16)
+        list3 = keep.tile([P, I // 16], U16)
+        lam_sb = keep.tile([P, PACK], F32)
+        kf_sb = keep.tile([P, PACK], F32)
+
+        nc.gpsimd.memset(wb_raw_plane[:].bitcast(I32), 0)
+
+        load_scale_rows(nc.sync, notes_plane, notes_scales, 0)
+        load_scale_rows(nc.sync, notes_plane, notes_scales, 1)
+        nc.sync.dma_start(out=wb_raw_codes[:].bitcast(I32),
+                          in_=wb_words[0].rearrange("p n t -> p (n t)").bitcast(I32))
+        nc.sync.dma_start(out=notes_codes[:].bitcast(I32), in_=notes_words[0].bitcast(I32))
+        for quadrant in range(4):
+            load_scale_rows(nc.scalar, wb_raw_plane, wb_scales, quadrant)
+        load_scale_rows(nc.sync, notes_plane, notes_scales, 2)
+        load_scale_rows(nc.sync, notes_plane, notes_scales, 3)
+        nc.sync.dma_start(list1[:], offs)
+        nc.sync.dma_start(list2[:], offs2)
+        nc.sync.dma_start(out=kf_sb[:], in_=kf.rearrange("(p t) o -> p (t o)", t=PACK))
+        nc.sync.dma_start(out=lam_sb[:], in_=lam.rearrange("(p t) o -> p (t o)", t=PACK))
+        nc.sync.dma_start(list3[:], offs3)
+        nc.sync.dma_start(out=wo_codes[:].bitcast(I32), in_=wo_words[0].bitcast(I32))
+        for quadrant in range(4):
+            load_scale_rows(nc.sync, wo_plane, wo_scales, quadrant)
+
+        f1 = [keep.tile([P, U], F32, name=f"f1_{t}", tag=f"f1_{t}") for t in range(PACK)]
+        for t in range(PACK):
+            nc.vector.memset(f1[t][:], 0.0)
+
+        first_codes = keep.tile([P, P], U32, align_bytes=64)
+        first_plane = keep.tile([P, P], U8, align_bytes=64)
+        rest_codes = keep.tile([P, PACK - 1, P], U32, align_bytes=64)
+        rest_plane = keep.tile([P, PACK - 1, P], U8, align_bytes=64)
+        nc.vector.tensor_copy(out=first_codes[:], in_=wb_raw_codes[:, 0::PACK])
+        nc.vector.tensor_copy(out=first_plane[:], in_=wb_raw_plane[:, 0::PACK])
+        for dealt, raw in ((rest_codes, wb_raw_codes), (rest_plane, wb_raw_plane)):
+            nc.vector.tensor_copy(out=dealt[:].rearrange("p t m -> p m t"),
+                                  in_=raw[:].rearrange("p (m t) -> p m t", t=PACK)[:, :, 1:])
+        wb_codes = [first_codes[:]] + [rest_codes[:, t, :] for t in range(PACK - 1)]
+        wb_plane = [first_plane[:]] + [rest_plane[:, t, :] for t in range(PACK - 1)]
+        banks = [[psum.tile([P, BANK], F32, name=f"bank{t}{b}", tag=f"bank{t}{b}") for b in range(2)]
+                 for t in range(PACK)]
+        for t in range(PACK):
+            for b in range(2):
+                nc.tensor.matmul_mx(
+                    out=banks[t][b][:],
+                    lhsT=wb_codes[t].bitcast(FP8X4), lhsT_scale=wb_plane[t],
+                    rhs=notes_codes[:, 2 * BANK * b : 2 * BANK * (b + 1)].bitcast(FP4X4),
+                    rhs_scale=notes_plane[:, BANK * b : BANK * (b + 1)],
+                    start=True, stop=True)
+
+        h1 = [keep.tile([P, U], F32, name=f"h1_{t}", tag=f"h1_{t}") for t in range(PACK)]
+        c1 = {}
+        picked = [keep.tile([P, I], F32, name=f"picked{t}", tag=f"picked{t}") for t in range(PACK)]
+        picked_kf = {}
+
+        def evacuate(engine, t, b):
+            dst = h1[t][:, BANK * b : BANK * (b + 1)]
+            if engine == "V":
+                nc.vector.tensor_copy(out=dst, in_=banks[t][b][:])
+            else:
+                nc.scalar.activation(dst, banks[t][b][:], COPY)
+
+        def pick(engine, t):
+            src = h1[t][:].indirect(list1[:])
+            if engine == "V":
+                nc.vector.tensor_copy(picked[t][:], src)
+            else:
+                nc.scalar.activation(picked[t][:], src, COPY)
+
+        def scale_picked(t, tag):
+            picked_kf[t] = keep.tile([P, I], F32, name=f"picked_kf{t}", tag=tag)
+            nc.gpsimd.tensor_scalar(picked_kf[t][:], picked[t][:], kf_sb[:, t : t + 1], 0.0, MULT, ADD)
+
+        def put_half(t, h):
+            nc.scalar.activation(f1[t][:].indirect(list2[:, 16 * h : 16 * (h + 1)]),
+                                 picked[t][:, HALF * h : HALF * (h + 1)], COPY)
+
+        def combine(engine, t, tag):
+            c1[t] = keep.tile([P, U], F32, name=f"c1_{t}", tag=tag)
+            if engine == "V":
+                for b in range(2):
+                    cols = slice(BANK * b, BANK * (b + 1))
+                    nc.vector.scalar_tensor_tensor(c1[t][:, cols], f1[t][:, cols], lam_sb[:, t : t + 1],
+                                                   banks[t][b][:], MULT, ADD)
+            else:
+                f1_lam = keep.tile([P, U], F32, name=f"f1_lam{t}", tag="f1_lam")
+                nc.gpsimd.tensor_scalar(f1_lam[:], f1[t][:], lam_sb[:, t : t + 1], 0.0, MULT, ADD)
+                nc.gpsimd.tensor_tensor(c1[t][:], f1_lam[:], h1[t][:], ADD)
+
+        evacuate("V", 0, 0)
+        evacuate("V", 0, 1)
+        pick("V", 0)
+        evacuate("S", 1, 0)
+        evacuate("S", 1, 1)
+        put_half(0, 0)
+        pick("S", 1)
+        put_half(0, 1)
+        scale_picked(0, "picked_kf0")
+        scale_picked(1, "picked_kf1")
+        evacuate("V", 2, 0)
+        evacuate("V", 2, 1)
+        evacuate("V", 3, 0)
+        pick("V", 2)
+        scale_picked(2, "picked_kf2")
+        for h in range(2):
+            put_half(1, h)
+            put_half(2, h)
+        evacuate("V", 3, 1)
+        pick("V", 3)
+        nc.vector.tensor_copy(f1[3][:].indirect(list2[:]), picked[3][:])
+        combine("G", 0, "h1_2")
+        scale_picked(3, "h1_0")
+        combine("G", 3, "c1_3")
+
+        third0 = keep.tile([P, I], F32)
+        nc.vector.tensor_copy(third0[:], c1[0][:].indirect(list3[:]))
+        combine("V", 1, "h1_2")
+        combine("V", 2, "f1_1")
+        third = keep.tile([P, PACK - 1, I], F32, tag="picked2")
+        thirds = [third0[:], third[:, 0, :], third[:, 1, :], third[:, 2, :]]
+        for t in (1, 3):
+            nc.scalar.activation(thirds[t], c1[t][:].indirect(list3[:]), COPY)
+        nc.scalar.activation(thirds[2][:, HALF:], c1[2][:].indirect(list3[:, 16:]), COPY)
+        w_planes = keep.tile([P, PACK, I], BF16, tag="f1_2")
+
+        def finish(t, cols):
+            nc.vector.scalar_tensor_tensor(w_planes[:, t, cols], thirds[t][:, cols], kf_sb[:, t : t + 1],
+                                           picked_kf[t][:, cols], MULT, SUB)
+
+        finish(0, slice(0, I))
+        nc.vector.tensor_copy(thirds[2][:, :HALF], c1[2][:].indirect(list3[:, :16]))
+        finish(1, slice(0, I))
+        finish(3, slice(0, I))
+        finish(2, slice(0, HALF))
+        finish(2, slice(HALF, I))
+
+        out_view = out.rearrange("(j p) i -> p j i", p=P)
+        for h in range(2):
+            cols = slice(HALF * h, HALF * (h + 1))
+            woven = keep.tile([P, HALF, PACK], BF16, align_bytes=64, name=f"woven{h}")
+            dst = woven[:].rearrange("p (c i) t -> p c t i", i=4)
+            src = w_planes[:, :, cols].rearrange("p t (c i) -> p c t i", i=4)
+            if h == 1:
+                nc.vector.tensor_copy(out=dst, in_=src)
+            else:
+                nc.scalar.copy(out=dst, in_=src)
+            w_codes = keep.tile([P, HALF], U32, align_bytes=64, name=f"w_codes{h}")
+            w_plane = keep.tile([P, HALF], U8, align_bytes=64, name=f"w_plane{h}")
+            nc.vector.quantize_mx(out=w_codes[:].bitcast(FP8X4), scales=w_plane[:],
+                                  in_=woven[:].rearrange("p i t -> p (i t)"))
+            result = keep.tile([P, 2, HALF], F32, name=f"result{h}")
+            for j in range(2):
+                acc = psum.tile([P, HALF], F32, name=f"acc{h}{j}", tag=f"bank{h}{j}")
+                nc.tensor.matmul_mx(
+                    out=acc[:],
+                    lhsT=wo_codes[:, 2 * P * j : 2 * P * (j + 1)].bitcast(FP4X4),
+                    lhsT_scale=wo_plane[:, P * j : P * (j + 1)],
+                    rhs=w_codes[:].bitcast(FP8X4), rhs_scale=w_plane[:],
+                    start=True, stop=True)
+                if j == 0:
+                    nc.vector.tensor_copy(out=result[:, j, :], in_=acc[:])
+                else:
+                    nc.scalar.activation(result[:, j, :], acc[:], COPY)
+            nc.sync.dma_start(out=out_view[:, :, cols], in_=result[:])

@@ -104,12 +104,12 @@ def tile_attend_hiddenhop_kernel(tc, notes_words, notes_scales, wb_words, wb_sca
             else:
                 nc.scalar.activation(dst, banks[t][b][:], COPY)
 
-        def pick(engine, t):
-            src = h1[t][:].indirect(list1[:])
+        def pick(engine, t, cols):
+            src = h1[t][:].indirect(list1[:, cols.start // 16 : cols.stop // 16])
             if engine == "V":
-                nc.vector.tensor_copy(picked[t][:], src)
+                nc.vector.tensor_copy(picked[t][:, cols], src)
             else:
-                nc.scalar.activation(picked[t][:], src, COPY)
+                nc.scalar.activation(picked[t][:, cols], src, COPY)
 
         def scale_picked(t, tag):
             picked_kf[t] = keep.tile([P, I], F32, name=f"picked_kf{t}", tag=tag)
@@ -119,64 +119,51 @@ def tile_attend_hiddenhop_kernel(tc, notes_words, notes_scales, wb_words, wb_sca
             nc.scalar.activation(f1[t][:].indirect(list2[:, 16 * h : 16 * (h + 1)]),
                                  picked[t][:, HALF * h : HALF * (h + 1)], COPY)
 
-        def combine(engine, t, tag):
+        def combine(t, tag):
             c1[t] = keep.tile([P, U], F32, name=f"c1_{t}", tag=tag)
-            if engine == "V":
-                for b in range(2):
-                    cols = slice(BANK * b, BANK * (b + 1))
-                    nc.vector.scalar_tensor_tensor(c1[t][:, cols], f1[t][:, cols], lam_sb[:, t : t + 1],
-                                                   banks[t][b][:], MULT, ADD)
-            else:
-                f1_lam = keep.tile([P, U], F32, name=f"f1_lam{t}", tag="f1_lam")
-                nc.gpsimd.tensor_scalar(f1_lam[:], f1[t][:], lam_sb[:, t : t + 1], 0.0, MULT, ADD)
-                nc.gpsimd.tensor_tensor(c1[t][:], f1_lam[:], h1[t][:], ADD)
+            for b in range(2):
+                cols = slice(BANK * b, BANK * (b + 1))
+                nc.vector.scalar_tensor_tensor(c1[t][:, cols], f1[t][:, cols], lam_sb[:, t : t + 1],
+                                               banks[t][b][:], MULT, ADD)
 
+        whole = slice(0, I)
+        halves = (slice(0, HALF), slice(HALF, I))
         evacuate("V", 0, 0)
         evacuate("V", 0, 1)
-        pick("V", 0)
+        pick("V", 0, whole)
         evacuate("S", 1, 0)
         evacuate("S", 1, 1)
         put_half(0, 0)
-        pick("S", 1)
+        pick("S", 1, whole)
         put_half(0, 1)
-        scale_picked(0, "picked_kf0")
         scale_picked(1, "picked_kf1")
         evacuate("V", 2, 0)
         evacuate("V", 2, 1)
         evacuate("V", 3, 0)
-        pick("V", 2)
+        pick("V", 2, whole)
         scale_picked(2, "picked_kf2")
         for h in range(2):
             put_half(1, h)
             put_half(2, h)
         evacuate("V", 3, 1)
-        pick("V", 3)
+        pick("V", 3, whole)
+        scale_picked(3, "picked_kf3")
+        combine(0, "h1_3")
         nc.vector.tensor_copy(f1[3][:].indirect(list2[:]), picked[3][:])
-        combine("G", 0, "h1_2")
-        scale_picked(3, "h1_0")
-        combine("G", 3, "c1_3")
+        v0 = keep.tile([P, I], F32, tag="picked3")
+        nc.vector.tensor_tensor(v0[:], c1[0][:].indirect(list3[:]), picked[0][:], SUB)
+        combine(1, "h1_3")
+        combine(3, "c1_3")
+        combine(2, "f1_3")
 
-        third0 = keep.tile([P, I], F32)
-        nc.vector.tensor_copy(third0[:], c1[0][:].indirect(list3[:]))
-        combine("V", 1, "h1_2")
-        combine("V", 2, "f1_1")
-        third = keep.tile([P, PACK - 1, I], F32, tag="picked2")
-        thirds = [third0[:], third[:, 0, :], third[:, 1, :], third[:, 2, :]]
-        for t in (1, 3):
-            nc.scalar.activation(thirds[t], c1[t][:].indirect(list3[:]), COPY)
-        nc.scalar.activation(thirds[2][:, HALF:], c1[2][:].indirect(list3[:, 16:]), COPY)
-        w_planes = keep.tile([P, PACK, I], BF16, tag="f1_2")
-
-        def finish(t, cols):
-            nc.vector.scalar_tensor_tensor(w_planes[:, t, cols], thirds[t][:, cols], kf_sb[:, t : t + 1],
+        w_planes = keep.tile([P, PACK, I], BF16, tag="picked2")
+        nc.scalar.activation(w_planes[:, 0, :], v0[:], COPY, scale=kf_sb[:, 0:1])
+        third = keep.tile([P, PACK - 1, I], F32)
+        for t, cols in ((1, whole), (3, whole), (2, halves[0]), (2, halves[1])):
+            nc.scalar.activation(third[:, t - 1, cols],
+                                 c1[t][:].indirect(list3[:, cols.start // 16 : cols.stop // 16]), COPY)
+            nc.vector.scalar_tensor_tensor(w_planes[:, t, cols], third[:, t - 1, cols], kf_sb[:, t : t + 1],
                                            picked_kf[t][:, cols], MULT, SUB)
-
-        finish(0, slice(0, I))
-        nc.vector.tensor_copy(thirds[2][:, :HALF], c1[2][:].indirect(list3[:, :16]))
-        finish(1, slice(0, I))
-        finish(3, slice(0, I))
-        finish(2, slice(0, HALF))
-        finish(2, slice(HALF, I))
 
         out_view = out.rearrange("(j p) i -> p j i", p=P)
         for h in range(2):

@@ -67,27 +67,22 @@ def tile_attend_hiddenhop_kernel(tc, notes_words, notes_scales, wb_words, wb_sca
             load_scale_rows(nc.sync, wo_plane, wo_scales, quadrant)
 
         f1 = [keep.tile([P, U], F32, name=f"f1_{t}", tag=f"f1_{t}") for t in range(PACK)]
-        for t in range(PACK):
+        nc.gpsimd.memset(f1[PACK - 1][:], 0.0)
+        for t in range(PACK - 1):
             nc.vector.memset(f1[t][:], 0.0)
 
-        first_codes = keep.tile([P, P], U32, align_bytes=64)
-        first_plane = keep.tile([P, P], U8, align_bytes=64)
-        rest_codes = keep.tile([P, PACK - 1, P], U32, align_bytes=64)
-        rest_plane = keep.tile([P, PACK - 1, P], U8, align_bytes=64)
-        nc.vector.tensor_copy(out=first_codes[:], in_=wb_raw_codes[:, 0::PACK])
-        nc.vector.tensor_copy(out=first_plane[:], in_=wb_raw_plane[:, 0::PACK])
-        for dealt, raw in ((rest_codes, wb_raw_codes), (rest_plane, wb_raw_plane)):
-            nc.vector.tensor_copy(out=dealt[:].rearrange("p t m -> p m t"),
-                                  in_=raw[:].rearrange("p (m t) -> p m t", t=PACK)[:, :, 1:])
-        wb_codes = [first_codes[:]] + [rest_codes[:, t, :] for t in range(PACK - 1)]
-        wb_plane = [first_plane[:]] + [rest_plane[:, t, :] for t in range(PACK - 1)]
+        wb_codes = [keep.tile([P, P], U32, align_bytes=64, name=f"wb_codes{t}") for t in range(PACK)]
+        wb_plane = [keep.tile([P, P], U8, align_bytes=64, name=f"wb_plane{t}") for t in range(PACK)]
+        for t in range(PACK):
+            nc.vector.tensor_copy(out=wb_codes[t][:], in_=wb_raw_codes[:, t::PACK])
+            nc.vector.tensor_copy(out=wb_plane[t][:], in_=wb_raw_plane[:, t::PACK])
         banks = [[psum.tile([P, BANK], F32, name=f"bank{t}{b}", tag=f"bank{t}{b}") for b in range(2)]
                  for t in range(PACK)]
         for t in range(PACK):
             for b in range(2):
                 nc.tensor.matmul_mx(
                     out=banks[t][b][:],
-                    lhsT=wb_codes[t].bitcast(FP8X4), lhsT_scale=wb_plane[t],
+                    lhsT=wb_codes[t][:].bitcast(FP8X4), lhsT_scale=wb_plane[t][:],
                     rhs=notes_codes[:, 2 * BANK * b : 2 * BANK * (b + 1)].bitcast(FP4X4),
                     rhs_scale=notes_plane[:, BANK * b : BANK * (b + 1)],
                     start=True, stop=True)
@@ -95,7 +90,6 @@ def tile_attend_hiddenhop_kernel(tc, notes_words, notes_scales, wb_words, wb_sca
         h1 = [keep.tile([P, U], F32, name=f"h1_{t}", tag=f"h1_{t}") for t in range(PACK)]
         c1 = {}
         picked = [keep.tile([P, I], F32, name=f"picked{t}", tag=f"picked{t}") for t in range(PACK)]
-        picked_kf = {}
 
         def evacuate(engine, t, b):
             dst = h1[t][:, BANK * b : BANK * (b + 1)]
@@ -110,10 +104,6 @@ def tile_attend_hiddenhop_kernel(tc, notes_words, notes_scales, wb_words, wb_sca
                 nc.vector.tensor_copy(picked[t][:, cols], src)
             else:
                 nc.scalar.activation(picked[t][:, cols], src, COPY)
-
-        def scale_picked(t, tag):
-            picked_kf[t] = keep.tile([P, I], F32, name=f"picked_kf{t}", tag=tag)
-            nc.gpsimd.tensor_scalar(picked_kf[t][:], picked[t][:], kf_sb[:, t : t + 1], 0.0, MULT, ADD)
 
         def put_half(t, h):
             nc.scalar.activation(f1[t][:].indirect(list2[:, 16 * h : 16 * (h + 1)]),
@@ -136,22 +126,22 @@ def tile_attend_hiddenhop_kernel(tc, notes_words, notes_scales, wb_words, wb_sca
         put_half(0, 0)
         pick("S", 1, whole)
         put_half(0, 1)
-        scale_picked(1, "picked_kf1")
         evacuate("V", 2, 0)
         evacuate("V", 2, 1)
         evacuate("V", 3, 0)
+        evacuate("V", 3, 1)
         pick("V", 2, whole)
-        scale_picked(2, "picked_kf2")
         for h in range(2):
             put_half(1, h)
             put_half(2, h)
-        evacuate("V", 3, 1)
         pick("V", 3, whole)
-        scale_picked(3, "picked_kf3")
         combine(0, "h1_3")
         nc.vector.tensor_copy(f1[3][:].indirect(list2[:]), picked[3][:])
-        v0 = keep.tile([P, I], F32, tag="picked3")
+        v0 = keep.tile([P, I], F32, tag="f1_0")
         nc.vector.tensor_tensor(v0[:], c1[0][:].indirect(list3[:]), picked[0][:], SUB)
+        picked_kf = keep.tile([P, PACK - 1, I], F32, tag="picked0")
+        for t in (2, 1, 3):
+            nc.gpsimd.tensor_scalar(picked_kf[:, t - 1, :], picked[t][:], kf_sb[:, t : t + 1], 0.0, MULT, ADD)
         combine(1, "h1_3")
         combine(3, "c1_3")
         combine(2, "f1_3")
@@ -163,9 +153,8 @@ def tile_attend_hiddenhop_kernel(tc, notes_words, notes_scales, wb_words, wb_sca
             nc.scalar.activation(third[:, t - 1, cols],
                                  c1[t][:].indirect(list3[:, cols.start // 16 : cols.stop // 16]), COPY)
             nc.vector.scalar_tensor_tensor(w_planes[:, t, cols], third[:, t - 1, cols], kf_sb[:, t : t + 1],
-                                           picked_kf[t][:, cols], MULT, SUB)
+                                           picked_kf[:, t - 1, cols], MULT, SUB)
 
-        out_view = out.rearrange("(j p) i -> p j i", p=P)
         for h in range(2):
             cols = slice(HALF * h, HALF * (h + 1))
             woven = keep.tile([P, HALF, PACK], BF16, align_bytes=64, name=f"woven{h}")
@@ -179,7 +168,6 @@ def tile_attend_hiddenhop_kernel(tc, notes_words, notes_scales, wb_words, wb_sca
             w_plane = keep.tile([P, HALF], U8, align_bytes=64, name=f"w_plane{h}")
             nc.vector.quantize_mx(out=w_codes[:].bitcast(FP8X4), scales=w_plane[:],
                                   in_=woven[:].rearrange("p i t -> p (i t)"))
-            result = keep.tile([P, 2, HALF], F32, name=f"result{h}")
             for j in range(2):
                 acc = psum.tile([P, HALF], F32, name=f"acc{h}{j}", tag=f"bank{h}{j}")
                 nc.tensor.matmul_mx(
@@ -188,8 +176,10 @@ def tile_attend_hiddenhop_kernel(tc, notes_words, notes_scales, wb_words, wb_sca
                     lhsT_scale=wo_plane[:, P * j : P * (j + 1)],
                     rhs=w_codes[:].bitcast(FP8X4), rhs_scale=w_plane[:],
                     start=True, stop=True)
+                result = keep.tile([P, HALF], F32, name=f"result{h}{j}")
                 if j == 0:
-                    nc.vector.tensor_copy(out=result[:, j, :], in_=acc[:])
+                    nc.vector.tensor_copy(out=result[:], in_=acc[:])
+                    nc.sync.dma_start(out=out[P * j : P * (j + 1), cols], in_=result[:])
                 else:
-                    nc.scalar.activation(result[:, j, :], acc[:], COPY)
-            nc.sync.dma_start(out=out_view[:, :, cols], in_=result[:])
+                    nc.scalar.activation(result[:], acc[:], COPY)
+                    nc.scalar.dma_start(out=out[P * j : P * (j + 1), cols], in_=result[:])

from contextlib import ExitStack

import concourse.mybir as mybir

D, K, U, I, E = 512, 512, 1024, 512, 256
P = 128
PACK = 4
BANK = 512
HALF = I // 2
FLOPS = 2 * D * K * U + 2 * K * E * I

F32 = mybir.dt.float32
BF16 = mybir.dt.bfloat16
I32 = mybir.dt.int32
U32 = mybir.dt.uint32
U16 = mybir.dt.uint16
U8 = mybir.dt.uint8
FP8X4 = mybir.dt.float8_e4m3fn_x4
FP4X4 = mybir.dt.float4_e2m1fn_x4
MULT = mybir.AluOpType.mult
ADD = mybir.AluOpType.add
SUB = mybir.AluOpType.subtract
COPY = mybir.ActivationFunctionType.Copy


def tile_attend_hiddenhop_kernel(tc, notes_words, notes_scales, wb_words, wb_scales, lam, kf,
                                  wo_words, wo_scales, offs, offs2, offs3, out):
    nc = tc.nc
    with ExitStack() as ctx:
        keep = ctx.enter_context(tc.tile_pool(name="keep", bufs=1))
        psum = ctx.enter_context(tc.psum_pool(name="psum", bufs=1))

        def load_scale_rows(queue, plane, scales, quadrant):
            queue.dma_start(out=plane[32 * quadrant : 32 * quadrant + 4, :].bitcast(I32),
                            in_=scales[0, 4 * quadrant : 4 * quadrant + 4, :].bitcast(I32))

        notes_codes = keep.tile([P, 2 * U], U8, align_bytes=64)
        notes_plane = keep.tile([P, U], U8, align_bytes=64)
        wb_raw_codes = keep.tile([P, K], U32, align_bytes=64)
        wb_raw_plane = keep.tile([P, K], U8, align_bytes=64)
        wo_codes = keep.tile([P, 2 * E], U8, align_bytes=64)
        wo_plane = keep.tile([P, E], U8, align_bytes=64)
        list1 = keep.tile([P, I // 16], U16)
        list2 = keep.tile([P, I // 16], U16)
        list3 = keep.tile([P, I // 16], U16)
        lam_sb = keep.tile([P, PACK], F32)
        kf_sb = keep.tile([P, PACK], F32)

        nc.gpsimd.memset(wb_raw_plane[:].bitcast(I32), 0)

        load_scale_rows(nc.sync, notes_plane, notes_scales, 0)
        load_scale_rows(nc.sync, notes_plane, notes_scales, 1)
        nc.sync.dma_start(out=wb_raw_codes[:].bitcast(I32),
                          in_=wb_words[0].rearrange("p n t -> p (n t)").bitcast(I32))
        nc.sync.dma_start(out=notes_codes[:].bitcast(I32), in_=notes_words[0].bitcast(I32))
        for quadrant in range(4):
            load_scale_rows(nc.scalar, wb_raw_plane, wb_scales, quadrant)
        load_scale_rows(nc.sync, notes_plane, notes_scales, 2)
        load_scale_rows(nc.sync, notes_plane, notes_scales, 3)
        nc.sync.dma_start(list1[:], offs)
        nc.sync.dma_start(list2[:], offs2)
        nc.sync.dma_start(out=kf_sb[:], in_=kf.rearrange("(p t) o -> p (t o)", t=PACK))
        nc.sync.dma_start(out=lam_sb[:], in_=lam.rearrange("(p t) o -> p (t o)", t=PACK))
        nc.sync.dma_start(list3[:], offs3)
        nc.sync.dma_start(out=wo_codes[:].bitcast(I32), in_=wo_words[0].bitcast(I32))
        for quadrant in range(4):
            load_scale_rows(nc.sync, wo_plane, wo_scales, quadrant)

        f1 = [keep.tile([P, U], F32, name=f"f1_{t}", tag=f"f1_{t}") for t in range(PACK)]
        nc.gpsimd.memset(f1[PACK - 1][:], 0.0)
        for t in range(PACK - 1):
            nc.vector.memset(f1[t][:], 0.0)

        wb_codes = [keep.tile([P, P], U32, align_bytes=64, name=f"wb_codes{t}") for t in range(PACK)]
        wb_plane = [keep.tile([P, P], U8, align_bytes=64, name=f"wb_plane{t}") for t in range(PACK)]
        for t in range(PACK):
            nc.vector.tensor_copy(out=wb_codes[t][:], in_=wb_raw_codes[:, t::PACK])
            nc.vector.tensor_copy(out=wb_plane[t][:], in_=wb_raw_plane[:, t::PACK])
        banks = [[psum.tile([P, BANK], F32, name=f"bank{t}{b}", tag=f"bank{t}{b}") for b in range(2)]
                 for t in range(PACK)]
        for t in range(PACK):
            for b in range(2):
                nc.tensor.matmul_mx(
                    out=banks[t][b][:],
                    lhsT=wb_codes[t][:].bitcast(FP8X4), lhsT_scale=wb_plane[t][:],
                    rhs=notes_codes[:, 2 * BANK * b : 2 * BANK * (b + 1)].bitcast(FP4X4),
                    rhs_scale=notes_plane[:, BANK * b : BANK * (b + 1)],
                    start=True, stop=True)

        h1 = [keep.tile([P, U], F32, name=f"h1_{t}", tag=f"h1_{t}") for t in range(PACK)]
        c1 = {}
        picked = [keep.tile([P, I], F32, name=f"picked{t}", tag=f"picked{t}") for t in range(PACK)]

        def evacuate(engine, t, b):
            dst = h1[t][:, BANK * b : BANK * (b + 1)]
            if engine == "V":
                nc.vector.tensor_copy(out=dst, in_=banks[t][b][:])
            else:
                nc.scalar.activation(dst, banks[t][b][:], COPY)

        def pick(engine, t, cols):
            src = h1[t][:].indirect(list1[:, cols.start // 16 : cols.stop // 16])
            if engine == "V":
                nc.vector.tensor_copy(picked[t][:, cols], src)
            else:
                nc.scalar.activation(picked[t][:, cols], src, COPY)

        def put_half(t, h):
            nc.scalar.activation(f1[t][:].indirect(list2[:, 16 * h : 16 * (h + 1)]),
                                 picked[t][:, HALF * h : HALF * (h + 1)], COPY)

        def combine(t, tag):
            c1[t] = keep.tile([P, U], F32, name=f"c1_{t}", tag=tag)
            for b in range(2):
                cols = slice(BANK * b, BANK * (b + 1))
                nc.vector.scalar_tensor_tensor(c1[t][:, cols], f1[t][:, cols], lam_sb[:, t : t + 1],
                                               banks[t][b][:], MULT, ADD)

        whole = slice(0, I)
        halves = (slice(0, HALF), slice(HALF, I))
        evacuate("V", 0, 0)
        evacuate("V", 0, 1)
        pick("V", 0, whole)
        evacuate("S", 1, 0)
        evacuate("S", 1, 1)
        put_half(0, 0)
        pick("S", 1, whole)
        put_half(0, 1)
        evacuate("V", 2, 0)
        evacuate("V", 2, 1)
        evacuate("V", 3, 0)
        evacuate("V", 3, 1)
        pick("V", 2, whole)
        for h in range(2):
            put_half(1, h)
            put_half(2, h)
        pick("V", 3, whole)
        combine(0, "h1_3")
        nc.vector.tensor_copy(f1[3][:].indirect(list2[:]), picked[3][:])
        v0 = keep.tile([P, I], F32, tag="f1_0")
        nc.vector.tensor_tensor(v0[:], c1[0][:].indirect(list3[:]), picked[0][:], SUB)
        picked_kf = keep.tile([P, PACK - 1, I], F32, tag="picked0")
        for t in (2, 1, 3):
            nc.gpsimd.tensor_scalar(picked_kf[:, t - 1, :], picked[t][:], kf_sb[:, t : t + 1], 0.0, MULT, ADD)
        combine(1, "h1_3")
        combine(3, "c1_3")
        combine(2, "f1_3")

        w_planes = keep.tile([P, PACK, I], BF16, tag="picked2")
        nc.scalar.activation(w_planes[:, 0, :], v0[:], COPY, scale=kf_sb[:, 0:1])
        third = keep.tile([P, PACK - 1, I], F32)
        for t, cols in ((1, whole), (3, whole), (2, halves[0]), (2, halves[1])):
            nc.scalar.activation(third[:, t - 1, cols],
                                 c1[t][:].indirect(list3[:, cols.start // 16 : cols.stop // 16]), COPY)
            nc.vector.scalar_tensor_tensor(w_planes[:, t, cols], third[:, t - 1, cols], kf_sb[:, t : t + 1],
                                           picked_kf[:, t - 1, cols], MULT, SUB)

        for h in range(2):
            cols = slice(HALF * h, HALF * (h + 1))
            woven = keep.tile([P, HALF, PACK], BF16, align_bytes=64, name=f"woven{h}")
            dst = woven[:].rearrange("p (c i) t -> p c t i", i=4)
            src = w_planes[:, :, cols].rearrange("p t (c i) -> p c t i", i=4)
            if h == 1:
                nc.vector.tensor_copy(out=dst, in_=src)
            else:
                nc.scalar.copy(out=dst, in_=src)
            w_codes = keep.tile([P, HALF], U32, align_bytes=64, name=f"w_codes{h}")
            w_plane = keep.tile([P, HALF], U8, align_bytes=64, name=f"w_plane{h}")
            nc.vector.quantize_mx(out=w_codes[:].bitcast(FP8X4), scales=w_plane[:],
                                  in_=woven[:].rearrange("p i t -> p (i t)"))
            for j in range(2):
                acc = psum.tile([P, HALF], F32, name=f"acc{h}{j}", tag=f"bank{h}{j}")
                nc.tensor.matmul_mx(
                    out=acc[:],
                    lhsT=wo_codes[:, 2 * P * j : 2 * P * (j + 1)].bitcast(FP4X4),
                    lhsT_scale=wo_plane[:, P * j : P * (j + 1)],
                    rhs=w_codes[:].bitcast(FP8X4), rhs_scale=w_plane[:],
                    start=True, stop=True)
                result = keep.tile([P, HALF], F32, name=f"result{h}{j}")
                if j == 0:
                    nc.vector.tensor_copy(out=result[:], in_=acc[:])
                    nc.sync.dma_start(out=out[P * j : P * (j + 1), cols], in_=result[:])
                else:
                    nc.scalar.activation(result[:], acc[:], COPY)
                    nc.scalar.dma_start(out=out[P * j : P * (j + 1), cols], in_=result[:])
